import numpy as np
import ml_dtypes


def mxq(x, axis, fmt="e4m3"):
    dtype, down = {"e4m3": (ml_dtypes.float8_e4m3fn, 7), "e5m2": (ml_dtypes.float8_e5m2, 14)}[fmt]
    v = np.moveaxis(np.asarray(x, np.float32).astype(ml_dtypes.bfloat16).astype(np.float64), axis, -1)
    blocks = v.reshape(v.shape[:-1] + (-1, 32))
    amax = np.abs(blocks).max(-1, keepdims=True)
    byte = np.maximum(np.where(amax > 0, np.frexp(amax)[1] - 1 + 127, 0) - down, 1)
    scale = np.exp2(byte - 127.0)
    codes = (blocks / scale).astype(np.float32).astype(dtype).astype(np.float64)
    return np.moveaxis((codes * scale).reshape(v.shape), -1, axis)


WIDE = False


def mx_kscale(k):
    if not WIDE:
        return np.ones(k)
    levels = np.array([10, -10, 5, -5, 0])
    if k % 512:
        return np.exp2(np.random.permutation(np.resize(levels, k // 32))).repeat(32)
    a = np.empty((k // 512, 16))
    for p in range(k // 512):
        a[p, :8] = np.random.permutation(np.resize(levels, 8))
        for g in range(8):
            far = levels[np.abs(levels - a[p, g]) >= 10]
            a[p, g + 8] = far[np.random.randint(len(far))]
    return np.exp2(a.ravel()).repeat(32)


def f64(x):
    return np.asarray(x).astype(np.float64)


def striped(idx):
    return np.tile(idx.reshape(-1, 16).T, (8, 1)).astype(np.uint16)


def unstriped(offs):
    return offs[:16].T.reshape(-1).astype(np.int64)


E2M1 = np.array([0.0, 0.5, 1.0, 1.5, 2.0, 3.0, 4.0, 6.0, -0.0, -0.5, -1.0, -1.5, -2.0, -3.0, -4.0, -6.0])


def pack_weight(w, fmt):
    k, n = w.shape
    w = f64(np.asarray(w, np.float32).astype(ml_dtypes.bfloat16)).reshape(k // 32, 32, n)
    amax = np.abs(w).max(1)
    if fmt == "e4m3":
        byte = np.frexp(amax)[1] - 1 + 127 - 7
    else:
        mant, ex = np.frexp(amax / 6.0)
        byte = np.where(mant > 0.5, ex, ex - 1) + 127
    byte = np.clip(np.where(amax > 0, byte, 1), 1, 254)
    scaled = (w * np.exp2(127.0 - byte)[:, None, :]).reshape(k, n).astype(np.float32)
    by_word = np.ascontiguousarray(scaled.reshape(k // 512, 128, 4, n).transpose(0, 1, 3, 2))
    if fmt == "e4m3":
        words = by_word.astype(ml_dtypes.float8_e4m3fn).view(np.uint8)
    else:
        c = by_word.astype(ml_dtypes.float4_e2m1fn).view(np.uint8) & 0xF
        words = (c[..., 0::2] | (c[..., 1::2] << 4)).reshape(k // 512, 128, 2 * n)
    return np.ascontiguousarray(words), np.ascontiguousarray(byte.astype(np.uint8).reshape(k // 512, 16, n))


def unpack_weight(words, scales, fmt):
    g, _, n = scales.shape
    words = np.ascontiguousarray(words).reshape(g, 128, n, -1)
    if fmt == "e4m3":
        vals = words.view(ml_dtypes.float8_e4m3fn).astype(np.float64)
    else:
        nib = np.empty((g, 128, n, 4), np.uint8)
        nib[..., 0::2] = words & 0xF
        nib[..., 1::2] = words >> 4
        vals = E2M1[nib]
    vals = vals * np.repeat(np.exp2(scales.astype(np.float64) - 127.0), 8, axis=1)[..., None]
    return vals.transpose(0, 1, 3, 2).reshape(g * 512, n)


def silu(v):
    return v / (1.0 + np.exp(-np.maximum(v, -700.0)))


K, T, E, C, H, N = 1024, 640, 4, 128, 512, 128


def by_expert(wq, xq):
    return np.concatenate([wq[e].T @ xq[:, e * C:(e + 1) * C] for e in range(E)], axis=1)


def setup_inputs():
    n = np.random.standard_normal
    s = mx_kscale(K)[:, None]
    u = mx_kscale(H)
    x = pack_weight(n((K, T)) * s, "e4m3")
    return {
        "x_words": x[0],
        "x_scales": x[1],
        "w1": (n((E + 1, K, H)) / np.sqrt(K) / s[None] * u[None, None, :]).astype(np.float32),
        "w2": (n((E + 1, H, N)) / np.sqrt(H) / u[None, :, None]).astype(np.float32),
        "gate": np.tile(np.random.uniform(0.2, 1.0, E * C), (N, 1)).astype(np.float32),
        "offs": striped(np.random.permutation(T)[:E * C]),
    }


def reference(x_words, x_scales, w1, w2, gate, offs):
    idx = unstriped(offs)
    w1q, w2q = mxq(f64(w1), 1, "e4m3"), mxq(f64(w2), 1, "e4m3")
    xs = unpack_weight(x_words, x_scales, "e4m3")
    hs = silu(w1q[E].T @ xs)
    ys = w2q[E].T @ mxq(hs, 0, "e4m3")
    xq = unpack_weight(x_words, x_scales, "e4m3")[:, idx]
    h = silu(by_expert(w1q, xq))
    y = by_expert(w2q, mxq(h, 0, "e4m3"))
    out = ys
    out[:, idx] += f64(gate) * y
    return out

@@ -1,0 +1,255 @@
+from contextlib import ExitStack
+
+import concourse.mybir as mybir
+
+K, T, E, C, H, N = 1024, 640, 4, 128, 512, 128
+FLOPS = 2 * (E * C + T) * (K * H + H * N)
+
+F32 = mybir.dt.float32
+BF16 = mybir.dt.bfloat16
+I32 = mybir.dt.int32
+U32 = mybir.dt.uint32
+U16 = mybir.dt.uint16
+U8 = mybir.dt.uint8
+FP8X4 = mybir.dt.float8_e4m3fn_x4
+SILU = mybir.ActivationFunctionType.Silu
+MULT = mybir.AluOpType.mult
+ADD = mybir.AluOpType.add
+
+P = 128
+PACK = 4
+K_PASS = P * PACK
+PASSES = K // K_PASS
+SHARED = E
+LAST = E - 1
+BLOCK = 128
+GATHER = 256
+
+
+def tile_moe_shr_mlp_silu_kernel(tc, x_words, x_scales, w1, w2, gate, offs, out):
+    nc = tc.nc
+    with ExitStack() as ctx:
+        keep = ctx.enter_context(tc.tile_pool(name="keep", bufs=1))
+        hid_psum = ctx.enter_context(tc.psum_pool(name="hid_psum", bufs=4))
+        y_psum = ctx.enter_context(tc.psum_pool(name="y_psum", bufs=2))
+        ys_psum = ctx.enter_context(tc.psum_pool(name="ys_psum", bufs=1))
+
+        def sb(name, shape, dtype, reuse=None):
+            return keep.tile(shape, dtype, name=name, tag=reuse or name, align_bytes=64)
+
+        def raw_name(e, o):
+            return "w1_raw%d_%d_%d" % (e, o, parts_of(e, o) - 1)
+
+        offsets = keep.tile([P, E * C // 16], U16, name="offsets")
+        x_scale = sb("x_scale", [P, T], U8)
+        nc.vector.memset(x_scale[:].bitcast(I32), 0)
+        warm = sb("warm", [P, 1], F32)
+        nc.vector.memset(warm[:], 0.0)
+        warm_out = sb("warm_out", [P, 1], F32)
+        routed = sb("routed", [P, T], F32)
+
+        x_word = []
+        for o in range(PASSES):
+            x_word.append(sb("x_word%d" % o, [P, T], I32))
+            nc.sync.dma_start(out=x_word[o][:], in_=x_words[o].rearrange("p t r -> p (t r)").bitcast(I32))
+            if o == 0:
+                nc.sync.dma_start(offsets[:], offs)
+        for q in range(4):
+            nc.scalar.dma_start(
+                out=x_scale[32 * q : 32 * q + 4 * PASSES, :].bitcast(I32),
+                in_=x_scales[:, 4 * q : 4 * q + 4, :].bitcast(I32),
+            )
+        nc.scalar.activation(warm_out[:], warm[:], SILU)
+
+        def parts_of(e, o):
+            return 2 if (e == LAST and o == PASSES - 1) else 1
+
+        w1_raw = {}
+        w2_raw = {}
+
+        def load_w1(e):
+            for o in range(PASSES):
+                rows = w1[e, o * K_PASS : (o + 1) * K_PASS, :].rearrange("(p j) c -> p j c", j=PACK)
+                width = H // parts_of(e, o)
+                for part in range(parts_of(e, o)):
+                    raw = sb("w1_raw%d_%d_%d" % (e, o, part), [P, PACK, width], F32)
+                    nc.sync.dma_start(out=raw[:], in_=rows[:, :, part * width : (part + 1) * width])
+                    w1_raw[e, o, part] = raw
+
+        def load_w2(e):
+            w2_raw[e] = sb("w2_raw%d" % e, [P, PACK, N], F32)
+            nc.sync.dma_start(out=w2_raw[e][:], in_=w2[e].rearrange("(p j) n -> p j n", j=PACK))
+
+        gate_sb = sb("gate_sb", [P, E * C], F32)
+        load_w1(SHARED)
+        for e in range(E):
+            load_w1(e)
+            load_w2(e)
+            if e == 0:
+                nc.sync.dma_start(out=gate_sb[:], in_=gate)
+        load_w2(SHARED)
+
+        slot_word = [sb("slot_word%d" % o, [P, E * C], U32) for o in range(PASSES)]
+        slot_scale = sb("slot_scale", [P, E * C], U8)
+
+        def gather_words(o, s0):
+            picked = offsets[:, s0 // 16 : (s0 + GATHER) // 16]
+            nc.vector.tensor_copy(slot_word[o][:, s0 : s0 + GATHER], x_word[o][:].bitcast(U32).indirect(picked))
+
+        def gather_scales(s0):
+            picked = offsets[:, s0 // 16 : (s0 + GATHER) // 16]
+            nc.vector.tensor_copy(slot_scale[:, s0 : s0 + GATHER], x_scale[:].indirect(picked))
+
+        w1_code = {}
+        w1_scale = {}
+
+        def prepare_w1(e, o):
+            parts = parts_of(e, o)
+            rows = P // parts
+            for pair in range(2):
+                w1_code[e, o, pair] = sb("w1_code%d_%d_%d" % (e, o, pair), [P, 2, P], U32)
+                w1_scale[e, o, pair] = sb("w1_scale%d_%d_%d" % (e, o, pair), [P, 2, P], U8)
+            for part in range(parts):
+                grouped = []
+                for pair in range(2):
+                    g = sb("w1_bf%d_%d_%d_%d" % (e, o, part, pair), [P, 2, rows, PACK], BF16)
+                    src = w1_raw[e, o, part][:].rearrange("p j (m t) -> p m j t", t=PACK)[:, :, :, 2 * pair : 2 * pair + 2]
+                    dst = g[:].rearrange("p t m j -> p m j t")
+                    if pair == 0:
+                        nc.vector.tensor_copy(dst, src)
+                    else:
+                        nc.scalar.copy(dst, src)
+                    grouped.append(g)
+                for pair in range(2):
+                    code, scale, g = w1_code[e, o, pair], w1_scale[e, o, pair], grouped[pair]
+                    if parts == 1:
+                        nc.vector.quantize_mx(
+                            out=code[:].rearrange("p t m -> p (t m)").bitcast(FP8X4),
+                            scales=scale[:].rearrange("p t m -> p (t m)"),
+                            in_=g[:].rearrange("p t m j -> p (t m j)"),
+                        )
+                    else:
+                        cols = slice(part * rows, (part + 1) * rows)
+                        for t in range(2):
+                            nc.vector.quantize_mx(
+                                out=code[:, t, cols].bitcast(FP8X4),
+                                scales=scale[:, t, cols],
+                                in_=g[:, t, :, :].rearrange("p m j -> p (m j)"),
+                            )
+
+        w2_code = {}
+        w2_scale = {}
+
+        def prepare_w2(e, on_scalar):
+            g = sb("w2_bf%d" % e, [P, N, PACK], BF16)
+            dst = g[:].rearrange("p (c i) j -> p c j i", i=4)
+            src = w2_raw[e][:].rearrange("p j (c i) -> p c j i", i=4)
+            if on_scalar:
+                nc.scalar.copy(dst, src)
+            else:
+                nc.vector.tensor_copy(dst, src)
+            w2_code[e] = sb("w2_code%d" % e, [P, N], U32)
+            w2_scale[e] = sb("w2_scale%d" % e, [P, N], U8)
+            nc.vector.quantize_mx(
+                out=w2_code[e][:].bitcast(FP8X4), scales=w2_scale[e][:], in_=g[:].rearrange("p n j -> p (n j)")
+            )
+
+        def hidden(e, words, scales, c0, h_bf, h_code, h_scale):
+            cols = slice(c0, c0 + BLOCK)
+            acc = hid_psum.tile([P, PACK, BLOCK], F32, name="acc")
+            for t in range(PACK):
+                for o in range(PASSES):
+                    nc.tensor.matmul_mx(
+                        out=acc[:, t, :],
+                        lhsT=w1_code[e, o, t // 2][:, t % 2, :].bitcast(FP8X4),
+                        lhsT_scale=w1_scale[e, o, t // 2][:, t % 2, :],
+                        rhs=words[o][:, cols].bitcast(FP8X4),
+                        rhs_scale=scales[4 * o : P, cols],
+                        start=(o == 0),
+                        stop=(o == PASSES - 1),
+                    )
+            nc.scalar.activation(h_bf, acc[:].rearrange("p t s -> p s t"), SILU)
+            nc.vector.quantize_mx(out=h_code.bitcast(FP8X4), scales=h_scale, in_=h_bf.rearrange("p s t -> p (s t)"))
+
+        for o in range(PASSES):
+            for s0 in range(0, E * C, GATHER):
+                gather_words(o, s0)
+        nc.vector.memset(routed[:], 0.0)
+        for s0 in range(0, E * C, GATHER):
+            gather_scales(s0)
+
+        hs_code = sb("hs_code", [P, T], U32)
+        hs_scale = sb("hs_scale", [P, T], U8)
+
+        def shared_hidden(block, h_bf):
+            cols = slice(block * BLOCK, (block + 1) * BLOCK)
+            hidden(SHARED, x_word, x_scale, block * BLOCK, h_bf, hs_code[:, cols], hs_scale[:, cols])
+
+        h_code = [sb("h_code%d" % e, [P, C], U32) for e in range(E)]
+        h_scale = [sb("h_scale%d" % e, [P, C], U8) for e in range(E)]
+
+        def routed_hidden(e, h_bf):
+            hidden(e, slot_word, slot_scale, e * C, h_bf, h_code[e][:], h_scale[e][:])
+
+        def h_pair(name, reuse):
+            return sb(name, [P, 2, BLOCK, PACK], BF16, reuse)
+
+        def second_layer(e, reuse):
+            y = y_psum.tile([P, C], F32, name="y")
+            nc.tensor.matmul_mx(
+                out=y[:],
+                lhsT=w2_code[e][:].bitcast(FP8X4),
+                lhsT_scale=w2_scale[e][:],
+                rhs=h_code[e][:].bitcast(FP8X4),
+                rhs_scale=h_scale[e][:],
+                start=True,
+                stop=True,
+            )
+            y_sb = sb("y_sb%d" % e, [P, C], F32, reuse)
+            nc.scalar.copy(y_sb[:], y[:])
+            slots = slice(e * C, (e + 1) * C)
+            picked = offsets[:, e * C // 16 : (e + 1) * C // 16]
+            nc.vector.tensor_tensor(routed[:].indirect(picked), y_sb[:], gate_sb[:, slots], MULT)
+
+        prepare_w1(SHARED, 0)
+        prepare_w1(SHARED, 1)
+        for o in range(PASSES):
+            prepare_w1(0, o)
+            pair = h_pair("hs_bf%d" % o, raw_name(0, o))
+            shared_hidden(2 * o, pair[:, 0, :, :])
+            shared_hidden(2 * o + 1, pair[:, 1, :, :])
+        for e in range(LAST):
+            prepare_w1(e + 1, 0)
+            pair = h_pair("h_bf%d" % e, raw_name(e + 1, 0))
+            if e == 0:
+                shared_hidden(4, pair[:, 1, :, :])
+            routed_hidden(e, pair[:, 0, :, :])
+            prepare_w2(e, False)
+            prepare_w1(e + 1, 1)
+            second_layer(e, raw_name(e + 1, 1))
+        prepare_w2(LAST, True)
+        routed_hidden(LAST, h_pair("h_bf%d" % LAST, None)[:, 0, :, :])
+        prepare_w2(SHARED, True)
+        second_layer(LAST, None)
+
+        result = []
+        for piece, (c0, widths) in enumerate(((0, (256, 128)), (384, (256,)))):
+            total = sum(widths)
+            ys = ys_psum.tile([P, total], F32, name="ys%d" % piece)
+            at = 0
+            for width in widths:
+                cols = slice(c0 + at, c0 + at + width)
+                nc.tensor.matmul_mx(
+                    out=ys[:, at : at + width],
+                    lhsT=w2_code[SHARED][:].bitcast(FP8X4),
+                    lhsT_scale=w2_scale[SHARED][:],
+                    rhs=hs_code[:, cols].bitcast(FP8X4),
+                    rhs_scale=hs_scale[:, cols],
+                    start=True,
+                    stop=True,
+                )
+                at = at + width
+            result.append(sb("result%d" % piece, [P, total], F32))
+            nc.vector.tensor_tensor(result[piece][:], ys[:], routed[:, c0 : c0 + total], ADD)
+            queue = nc.sync if piece == 0 else nc.scalar
+            queue.dma_start(out=out[:, c0 : c0 + total], in_=result[piece][:])

@@ -1,6 +1,7 @@
 from contextlib import ExitStack
 
 import concourse.mybir as mybir
+from concourse.masks import make_identity
 
 K, T, E, C, H, N = 1024, 640, 4, 128, 512, 128
 FLOPS = 2 * (E * C + T) * (K * H + H * N)
@@ -37,219 +38,217 @@ def tile_moe_shr_mlp_silu_kernel(tc, x_words, x_scales, w1, w2, gate, offs, out)
         def sb(name, shape, dtype, reuse=None):
             return keep.tile(shape, dtype, name=name, tag=reuse or name, align_bytes=64)
 
-        def raw_name(e, o):
-            return "w1_raw%d_%d_%d" % (e, o, parts_of(e, o) - 1)
-
         offsets = keep.tile([P, E * C // 16], U16, name="offsets")
         x_scale = sb("x_scale", [P, T], U8)
-        nc.vector.memset(x_scale[:].bitcast(I32), 0)
+        nc.gpsimd.memset(x_scale[:].bitcast(I32), 0)
+        gate_rows = sb("gate_rows", [P, C], F32)
+        nc.gpsimd.memset(gate_rows[:], 0.0)
+        warm_out = sb("warm_out", [P, 1], F32)
         warm = sb("warm", [P, 1], F32)
         nc.vector.memset(warm[:], 0.0)
-        warm_out = sb("warm_out", [P, 1], F32)
         routed = sb("routed", [P, T], F32)
+        nc.vector.memset(routed[:], 0.0)
+        identity = sb("identity", [P, P], F32)
+        make_identity(nc, identity[:])
 
-        x_word = []
-        for o in range(PASSES):
-            x_word.append(sb("x_word%d" % o, [P, T], I32))
+        nc.scalar.activation(warm_out[:], warm[:], SILU)
+        x_word = [sb("x_word%d" % o, [P, T], I32) for o in range(PASSES)]
+
+        def load_words(o):
             nc.sync.dma_start(out=x_word[o][:], in_=x_words[o].rearrange("p t r -> p (t r)").bitcast(I32))
-            if o == 0:
-                nc.sync.dma_start(offsets[:], offs)
+
+        load_words(0)
         for q in range(4):
-            nc.scalar.dma_start(
+            nc.sync.dma_start(
                 out=x_scale[32 * q : 32 * q + 4 * PASSES, :].bitcast(I32),
                 in_=x_scales[:, 4 * q : 4 * q + 4, :].bitcast(I32),
             )
-        nc.scalar.activation(warm_out[:], warm[:], SILU)
-
-        def parts_of(e, o):
-            return 2 if (e == LAST and o == PASSES - 1) else 1
+        nc.sync.dma_start(out=gate_rows[0:E, :], in_=gate[0].rearrange("(e c) -> e c", c=C))
+        nc.sync.dma_start(offsets[:], offs)
 
         w1_raw = {}
         w2_raw = {}
 
-        def load_w1(e):
-            for o in range(PASSES):
-                rows = w1[e, o * K_PASS : (o + 1) * K_PASS, :].rearrange("(p j) c -> p j c", j=PACK)
-                width = H // parts_of(e, o)
-                for part in range(parts_of(e, o)):
-                    raw = sb("w1_raw%d_%d_%d" % (e, o, part), [P, PACK, width], F32)
-                    nc.sync.dma_start(out=raw[:], in_=rows[:, :, part * width : (part + 1) * width])
-                    w1_raw[e, o, part] = raw
+        def raw_name(e, o):
+            return "w1_raw%d_%d" % (e, o)
+
+        def bf_name(e, o, pair):
+            return "w1_bf%d_%d_%d" % (e, o, pair)
+
+        def load_w1(e, o):
+            w1_raw[e, o] = sb(raw_name(e, o), [P, PACK, H], F32)
+            rows = w1[e, o * K_PASS : (o + 1) * K_PASS, :]
+            nc.sync.dma_start(out=w1_raw[e, o][:], in_=rows.rearrange("(p j) c -> p j c", j=PACK))
 
         def load_w2(e):
             w2_raw[e] = sb("w2_raw%d" % e, [P, PACK, N], F32)
             nc.sync.dma_start(out=w2_raw[e][:], in_=w2[e].rearrange("(p j) n -> p j n", j=PACK))
 
-        gate_sb = sb("gate_sb", [P, E * C], F32)
-        load_w1(SHARED)
-        for e in range(E):
-            load_w1(e)
+        load_w1(SHARED, 0)
+        load_words(1)
+        load_w1(SHARED, 1)
+        load_w1(0, 0)
+        load_w1(0, 1)
+        for e in range(1, LAST):
+            load_w1(e, 0)
+            load_w2(e - 1)
+            load_w1(e, 1)
+        load_w1(LAST, 0)
+        load_w1(LAST, 1)
+        for e in (LAST - 1, LAST, SHARED):
             load_w2(e)
-            if e == 0:
-                nc.sync.dma_start(out=gate_sb[:], in_=gate)
-        load_w2(SHARED)
+
+        gate_cols_psum = y_psum.tile([P, P], F32, name="y")
+        nc.tensor.transpose(gate_cols_psum[:], gate_rows[:], identity[:])
+        gate_cols = sb("gate_cols", [P, E], F32)
+        nc.scalar.copy(gate_cols[:], gate_cols_psum[:, 0:E])
+        gate_psum = hid_psum.tile([P, E, C], F32, name="acc")
+        for e in range(E):
+            nc.tensor.transpose(gate_psum[:, e, :], gate_cols[:, e : e + 1].to_broadcast([P, P]), identity[:])
+        gate_sb = sb("gate_sb", [P, E, C], F32)
+        nc.scalar.copy(gate_sb[:], gate_psum[:])
 
         slot_word = [sb("slot_word%d" % o, [P, E * C], U32) for o in range(PASSES)]
         slot_scale = sb("slot_scale", [P, E * C], U8)
+        for window, gathered in ((x_word[0][:].bitcast(U32), slot_word[0]), (x_scale[:], slot_scale), (x_word[1][:].bitcast(U32), slot_word[1])):
+            for s0 in range(0, E * C, GATHER):
+                picked = offsets[:, s0 // 16 : (s0 + GATHER) // 16]
+                nc.vector.tensor_copy(gathered[:, s0 : s0 + GATHER], window.indirect(picked))
 
-        def gather_words(o, s0):
-            picked = offsets[:, s0 // 16 : (s0 + GATHER) // 16]
-            nc.vector.tensor_copy(slot_word[o][:, s0 : s0 + GATHER], x_word[o][:].bitcast(U32).indirect(picked))
-
-        def gather_scales(s0):
-            picked = offsets[:, s0 // 16 : (s0 + GATHER) // 16]
-            nc.vector.tensor_copy(slot_scale[:, s0 : s0 + GATHER], x_scale[:].indirect(picked))
+        def quantize(code, scale, values):
+            nc.vector.quantize_mx(out=code.bitcast(FP8X4), scales=scale, in_=values)
 
         w1_code = {}
         w1_scale = {}
 
-        def prepare_w1(e, o):
-            parts = parts_of(e, o)
-            rows = P // parts
+        def prepare_w1(e, o, vector_alone=False):
+            grouped = []
             for pair in range(2):
-                w1_code[e, o, pair] = sb("w1_code%d_%d_%d" % (e, o, pair), [P, 2, P], U32)
-                w1_scale[e, o, pair] = sb("w1_scale%d_%d_%d" % (e, o, pair), [P, 2, P], U8)
-            for part in range(parts):
-                grouped = []
-                for pair in range(2):
-                    g = sb("w1_bf%d_%d_%d_%d" % (e, o, part, pair), [P, 2, rows, PACK], BF16)
-                    src = w1_raw[e, o, part][:].rearrange("p j (m t) -> p m j t", t=PACK)[:, :, :, 2 * pair : 2 * pair + 2]
-                    dst = g[:].rearrange("p t m j -> p m j t")
-                    if pair == 0:
-                        nc.vector.tensor_copy(dst, src)
-                    else:
-                        nc.scalar.copy(dst, src)
-                    grouped.append(g)
-                for pair in range(2):
-                    code, scale, g = w1_code[e, o, pair], w1_scale[e, o, pair], grouped[pair]
-                    if parts == 1:
-                        nc.vector.quantize_mx(
-                            out=code[:].rearrange("p t m -> p (t m)").bitcast(FP8X4),
-                            scales=scale[:].rearrange("p t m -> p (t m)"),
-                            in_=g[:].rearrange("p t m j -> p (t m j)"),
-                        )
-                    else:
-                        cols = slice(part * rows, (part + 1) * rows)
-                        for t in range(2):
-                            nc.vector.quantize_mx(
-                                out=code[:, t, cols].bitcast(FP8X4),
-                                scales=scale[:, t, cols],
-                                in_=g[:, t, :, :].rearrange("p m j -> p (m j)"),
-                            )
+                g = sb(bf_name(e, o, pair), [P, 2, P, PACK], BF16)
+                src = w1_raw[e, o][:].rearrange("p j (m t) -> p m j t", t=PACK)[:, :, :, 2 * pair : 2 * pair + 2]
+                dst = g[:].rearrange("p t m j -> p m j t")
+                if pair == 0 or vector_alone:
+                    nc.vector.tensor_copy(dst, src)
+                else:
+                    nc.scalar.copy(dst, src)
+                grouped.append(g)
+            for pair in range(2):
+                w1_code[e, o, pair] = sb("w1_code%d_%d_%d" % (e, o, pair), [P, 2 * P], U32)
+                w1_scale[e, o, pair] = sb("w1_scale%d_%d_%d" % (e, o, pair), [P, 2 * P], U8)
+                values = grouped[pair][:].rearrange("p t m j -> p (t m j)")
+                quantize(w1_code[e, o, pair][:], w1_scale[e, o, pair][:], values)
 
         w2_code = {}
         w2_scale = {}
 
-        def prepare_w2(e, on_scalar):
+        def prepare_w2(e):
             g = sb("w2_bf%d" % e, [P, N, PACK], BF16)
             dst = g[:].rearrange("p (c i) j -> p c j i", i=4)
             src = w2_raw[e][:].rearrange("p j (c i) -> p c j i", i=4)
-            if on_scalar:
-                nc.scalar.copy(dst, src)
-            else:
-                nc.vector.tensor_copy(dst, src)
+            nc.scalar.copy(dst, src)
             w2_code[e] = sb("w2_code%d" % e, [P, N], U32)
             w2_scale[e] = sb("w2_scale%d" % e, [P, N], U8)
-            nc.vector.quantize_mx(
-                out=w2_code[e][:].bitcast(FP8X4), scales=w2_scale[e][:], in_=g[:].rearrange("p n j -> p (n j)")
-            )
+            quantize(w2_code[e][:], w2_scale[e][:], g[:].rearrange("p n j -> p (n j)"))
 
-        def hidden(e, words, scales, c0, h_bf, h_code, h_scale):
+        def hidden(e, words, scales, c0, h_bf):
             cols = slice(c0, c0 + BLOCK)
             acc = hid_psum.tile([P, PACK, BLOCK], F32, name="acc")
             for t in range(PACK):
+                w_cols = slice((t % 2) * P, (t % 2 + 1) * P)
                 for o in range(PASSES):
                     nc.tensor.matmul_mx(
                         out=acc[:, t, :],
-                        lhsT=w1_code[e, o, t // 2][:, t % 2, :].bitcast(FP8X4),
-                        lhsT_scale=w1_scale[e, o, t // 2][:, t % 2, :],
+                        lhsT=w1_code[e, o, t // 2][:, w_cols].bitcast(FP8X4),
+                        lhsT_scale=w1_scale[e, o, t // 2][:, w_cols],
                         rhs=words[o][:, cols].bitcast(FP8X4),
                         rhs_scale=scales[4 * o : P, cols],
                         start=(o == 0),
                         stop=(o == PASSES - 1),
                     )
             nc.scalar.activation(h_bf, acc[:].rearrange("p t s -> p s t"), SILU)
-            nc.vector.quantize_mx(out=h_code.bitcast(FP8X4), scales=h_scale, in_=h_bf.rearrange("p s t -> p (s t)"))
-
-        for o in range(PASSES):
-            for s0 in range(0, E * C, GATHER):
-                gather_words(o, s0)
-        nc.vector.memset(routed[:], 0.0)
-        for s0 in range(0, E * C, GATHER):
-            gather_scales(s0)
-
-        hs_code = sb("hs_code", [P, T], U32)
-        hs_scale = sb("hs_scale", [P, T], U8)
 
         def shared_hidden(block, h_bf):
-            cols = slice(block * BLOCK, (block + 1) * BLOCK)
-            hidden(SHARED, x_word, x_scale, block * BLOCK, h_bf, hs_code[:, cols], hs_scale[:, cols])
-
-        h_code = [sb("h_code%d" % e, [P, C], U32) for e in range(E)]
-        h_scale = [sb("h_scale%d" % e, [P, C], U8) for e in range(E)]
+            hidden(SHARED, x_word, x_scale, block * BLOCK, h_bf)
 
         def routed_hidden(e, h_bf):
-            hidden(e, slot_word, slot_scale, e * C, h_bf, h_code[e][:], h_scale[e][:])
+            hidden(e, slot_word, slot_scale, e * C, h_bf)
 
-        def h_pair(name, reuse):
-            return sb(name, [P, 2, BLOCK, PACK], BF16, reuse)
+        def h_tile(name, blocks, reuse):
+            return sb(name, [P, blocks, BLOCK, PACK], BF16, reuse)
 
-        def second_layer(e, reuse):
-            y = y_psum.tile([P, C], F32, name="y")
+        def quantize_h(name, h_bf, blocks, reuse=None):
+            code = sb(name + "_code", [P, blocks * BLOCK], U32, reuse)
+            scale = sb(name + "_scale", [P, blocks * BLOCK], U8)
+            quantize(code[:], scale[:], h_bf[:].rearrange("p b s t -> p (b s t)"))
+            return code, scale
+
+        def second_matmul(e, y, h_code, h_scale):
             nc.tensor.matmul_mx(
-                out=y[:],
+                out=y,
                 lhsT=w2_code[e][:].bitcast(FP8X4),
                 lhsT_scale=w2_scale[e][:],
-                rhs=h_code[e][:].bitcast(FP8X4),
-                rhs_scale=h_scale[e][:],
+                rhs=h_code.bitcast(FP8X4),
+                rhs_scale=h_scale,
                 start=True,
                 stop=True,
             )
+
+        def routed_output(e, h_code, h_scale, reuse):
+            y = y_psum.tile([P, C], F32, name="y")
+            second_matmul(e, y[:], h_code, h_scale)
             y_sb = sb("y_sb%d" % e, [P, C], F32, reuse)
             nc.scalar.copy(y_sb[:], y[:])
-            slots = slice(e * C, (e + 1) * C)
             picked = offsets[:, e * C // 16 : (e + 1) * C // 16]
-            nc.vector.tensor_tensor(routed[:].indirect(picked), y_sb[:], gate_sb[:, slots], MULT)
+            nc.vector.tensor_tensor(routed[:].indirect(picked), y_sb[:], gate_sb[:, e, :], MULT)
 
         prepare_w1(SHARED, 0)
         prepare_w1(SHARED, 1)
+        hs = []
+        waiting = None
         for o in range(PASSES):
-            prepare_w1(0, o)
-            pair = h_pair("hs_bf%d" % o, raw_name(0, o))
-            shared_hidden(2 * o, pair[:, 0, :, :])
-            shared_hidden(2 * o + 1, pair[:, 1, :, :])
-        for e in range(LAST):
-            prepare_w1(e + 1, 0)
-            pair = h_pair("h_bf%d" % e, raw_name(e + 1, 0))
+            prepare_w1(0, o, vector_alone=(o == 1))
+            if waiting is not None:
+                hs.append(quantize_h("hs%d" % (o - 1), waiting, 2, bf_name(0, o, 1)))
+            waiting = h_tile("hs_bf%d" % o, 2, raw_name(0, o))
+            shared_hidden(2 * o, waiting[:, 0, :, :])
+            shared_hidden(2 * o + 1, waiting[:, 1, :, :])
+        for e in range(LAST - 1):
+            prepare_w1(e + 1, 0, vector_alone=(e == 0))
+            blocks = 2 if e == 0 else 1
+            h_bf = h_tile("h_bf%d" % e, blocks, raw_name(e + 1, 0))
             if e == 0:
-                shared_hidden(4, pair[:, 1, :, :])
-            routed_hidden(e, pair[:, 0, :, :])
-            prepare_w2(e, False)
+                hs.append(quantize_h("hs1", waiting, 2, bf_name(1, 0, 1)))
+                shared_hidden(4, h_bf[:, 1, :, :])
+            routed_hidden(e, h_bf[:, 0, :, :])
+            code, scale = quantize_h("h%d" % e, h_bf, blocks)
+            if e == 0:
+                hs.append((code[:, BLOCK:], scale[:, BLOCK:]))
+            prepare_w2(e)
             prepare_w1(e + 1, 1)
-            second_layer(e, raw_name(e + 1, 1))
-        prepare_w2(LAST, True)
-        routed_hidden(LAST, h_pair("h_bf%d" % LAST, None)[:, 0, :, :])
-        prepare_w2(SHARED, True)
-        second_layer(LAST, None)
+            routed_output(e, code[:, :C], scale[:, :C], raw_name(e + 1, 1))
 
-        result = []
-        for piece, (c0, widths) in enumerate(((0, (256, 128)), (384, (256,)))):
-            total = sum(widths)
-            ys = ys_psum.tile([P, total], F32, name="ys%d" % piece)
-            at = 0
-            for width in widths:
-                cols = slice(c0 + at, c0 + at + width)
-                nc.tensor.matmul_mx(
-                    out=ys[:, at : at + width],
-                    lhsT=w2_code[SHARED][:].bitcast(FP8X4),
-                    lhsT_scale=w2_scale[SHARED][:],
-                    rhs=hs_code[:, cols].bitcast(FP8X4),
-                    rhs_scale=hs_scale[:, cols],
-                    start=True,
-                    stop=True,
-                )
-                at = at + width
-            result.append(sb("result%d" % piece, [P, total], F32))
-            nc.vector.tensor_tensor(result[piece][:], ys[:], routed[:, c0 : c0 + total], ADD)
-            queue = nc.sync if piece == 0 else nc.scalar
-            queue.dma_start(out=out[:, c0 : c0 + total], in_=result[piece][:])
+        e = LAST - 1
+        prepare_w1(LAST, 0)
+        h_bf = h_tile("h_bf%d" % e, 1, raw_name(LAST, 0))
+        routed_hidden(e, h_bf[:, 0, :, :])
+        prepare_w1(LAST, 1)
+        code, scale = quantize_h("h%d" % e, h_bf, 1, bf_name(LAST, 1, 1))
+        prepare_w2(e)
+        routed_output(e, code[:], scale[:], None)
+        prepare_w2(LAST)
+        h_bf = h_tile("h_bf%d" % LAST, 1, None)
+        routed_hidden(LAST, h_bf[:, 0, :, :])
+        code, scale = quantize_h("h%d" % LAST, h_bf, 1)
+        prepare_w2(SHARED)
+        routed_output(LAST, code[:], scale[:], None)
+
+        ys = [ys_psum.tile([P, 4 * BLOCK], F32, name="ys_a"), ys_psum.tile([P, BLOCK], F32, name="ys_b")]
+        pieces = [(0, ys[0][:, : 2 * BLOCK]), (2 * BLOCK, ys[0][:, 2 * BLOCK :]), (4 * BLOCK, ys[1][:])]
+        for (c0, y), (code, scale) in zip(pieces, hs):
+            second_matmul(SHARED, y, code[:], scale[:])
+        for piece, (c0, y) in enumerate(pieces):
+            width = y.shape[1]
+            result = sb("result%d" % piece, [P, width], F32)
+            nc.vector.tensor_tensor(result[:], y, routed[:, c0 : c0 + width], ADD)
+            queue = nc.scalar if piece == 1 else nc.sync
+            queue.dma_start(out=out[:, c0 : c0 + width], in_=result[:])

@@ -31,7 +31,7 @@ def tile_moe_shr_mlp_silu_kernel(tc, x_words, x_scales, w1, w2, gate, offs, out)
     nc = tc.nc
     with ExitStack() as ctx:
         keep = ctx.enter_context(tc.tile_pool(name="keep", bufs=1))
-        hid_psum = ctx.enter_context(tc.psum_pool(name="hid_psum", bufs=4))
+        hid_psum = ctx.enter_context(tc.psum_pool(name="hid_psum", bufs=1))
         y_psum = ctx.enter_context(tc.psum_pool(name="y_psum", bufs=2))
         ys_psum = ctx.enter_context(tc.psum_pool(name="ys_psum", bufs=1))
 
@@ -40,9 +40,9 @@ def tile_moe_shr_mlp_silu_kernel(tc, x_words, x_scales, w1, w2, gate, offs, out)
 
         offsets = keep.tile([P, E * C // 16], U16, name="offsets")
         x_scale = sb("x_scale", [P, T], U8)
-        nc.gpsimd.memset(x_scale[:].bitcast(I32), 0)
+        nc.vector.memset(x_scale[:].bitcast(I32), 0)
         gate_rows = sb("gate_rows", [P, C], F32)
-        nc.gpsimd.memset(gate_rows[:], 0.0)
+        nc.vector.memset(gate_rows[:], 0.0)
         warm_out = sb("warm_out", [P, 1], F32)
         warm = sb("warm", [P, 1], F32)
         nc.vector.memset(warm[:], 0.0)
@@ -51,20 +51,20 @@ def tile_moe_shr_mlp_silu_kernel(tc, x_words, x_scales, w1, w2, gate, offs, out)
         identity = sb("identity", [P, P], F32)
         make_identity(nc, identity[:])
 
-        nc.scalar.activation(warm_out[:], warm[:], SILU)
         x_word = [sb("x_word%d" % o, [P, T], I32) for o in range(PASSES)]
 
         def load_words(o):
             nc.sync.dma_start(out=x_word[o][:], in_=x_words[o].rearrange("p t r -> p (t r)").bitcast(I32))
 
         load_words(0)
+        nc.sync.dma_start(offsets[:], offs)
+        load_words(1)
         for q in range(4):
-            nc.sync.dma_start(
+            nc.scalar.dma_start(
                 out=x_scale[32 * q : 32 * q + 4 * PASSES, :].bitcast(I32),
                 in_=x_scales[:, 4 * q : 4 * q + 4, :].bitcast(I32),
             )
-        nc.sync.dma_start(out=gate_rows[0:E, :], in_=gate[0].rearrange("(e c) -> e c", c=C))
-        nc.sync.dma_start(offsets[:], offs)
+        nc.scalar.activation(warm_out[:], warm[:], SILU)
 
         w1_raw = {}
         w2_raw = {}
@@ -85,9 +85,9 @@ def tile_moe_shr_mlp_silu_kernel(tc, x_words, x_scales, w1, w2, gate, offs, out)
             nc.sync.dma_start(out=w2_raw[e][:], in_=w2[e].rearrange("(p j) n -> p j n", j=PACK))
 
         load_w1(SHARED, 0)
-        load_words(1)
         load_w1(SHARED, 1)
         load_w1(0, 0)
+        nc.sync.dma_start(out=gate_rows[0:E, :], in_=gate[0].rearrange("(e c) -> e c", c=C))
         load_w1(0, 1)
         for e in range(1, LAST):
             load_w1(e, 0)
@@ -98,19 +98,9 @@ def tile_moe_shr_mlp_silu_kernel(tc, x_words, x_scales, w1, w2, gate, offs, out)
         for e in (LAST - 1, LAST, SHARED):
             load_w2(e)
 
-        gate_cols_psum = y_psum.tile([P, P], F32, name="y")
-        nc.tensor.transpose(gate_cols_psum[:], gate_rows[:], identity[:])
-        gate_cols = sb("gate_cols", [P, E], F32)
-        nc.scalar.copy(gate_cols[:], gate_cols_psum[:, 0:E])
-        gate_psum = hid_psum.tile([P, E, C], F32, name="acc")
-        for e in range(E):
-            nc.tensor.transpose(gate_psum[:, e, :], gate_cols[:, e : e + 1].to_broadcast([P, P]), identity[:])
-        gate_sb = sb("gate_sb", [P, E, C], F32)
-        nc.scalar.copy(gate_sb[:], gate_psum[:])
-
         slot_word = [sb("slot_word%d" % o, [P, E * C], U32) for o in range(PASSES)]
         slot_scale = sb("slot_scale", [P, E * C], U8)
-        for window, gathered in ((x_word[0][:].bitcast(U32), slot_word[0]), (x_scale[:], slot_scale), (x_word[1][:].bitcast(U32), slot_word[1])):
+        for window, gathered in ((x_word[0][:].bitcast(U32), slot_word[0]), (x_word[1][:].bitcast(U32), slot_word[1]), (x_scale[:], slot_scale)):
             for s0 in range(0, E * C, GATHER):
                 picked = offsets[:, s0 // 16 : (s0 + GATHER) // 16]
                 nc.vector.tensor_copy(gathered[:, s0 : s0 + GATHER], window.indirect(picked))
@@ -141,37 +131,40 @@ def tile_moe_shr_mlp_silu_kernel(tc, x_words, x_scales, w1, w2, gate, offs, out)
         w2_code = {}
         w2_scale = {}
 
-        def prepare_w2(e):
+        def prepare_w2(e, copy):
             g = sb("w2_bf%d" % e, [P, N, PACK], BF16)
             dst = g[:].rearrange("p (c i) j -> p c j i", i=4)
             src = w2_raw[e][:].rearrange("p j (c i) -> p c j i", i=4)
-            nc.scalar.copy(dst, src)
+            copy(dst, src)
             w2_code[e] = sb("w2_code%d" % e, [P, N], U32)
             w2_scale[e] = sb("w2_scale%d" % e, [P, N], U8)
             quantize(w2_code[e][:], w2_scale[e][:], g[:].rearrange("p n j -> p (n j)"))
 
-        def hidden(e, words, scales, c0, h_bf):
+        def first_matmul(e, t, o, acc, words, scales, cols):
+            w_cols = slice((t % 2) * P, (t % 2 + 1) * P)
+            nc.tensor.matmul_mx(
+                out=acc,
+                lhsT=w1_code[e, o, t // 2][:, w_cols].bitcast(FP8X4),
+                lhsT_scale=w1_scale[e, o, t // 2][:, w_cols],
+                rhs=words[o][:, cols].bitcast(FP8X4),
+                rhs_scale=scales[4 * o : P, cols],
+                start=(o == 0),
+                stop=(o == PASSES - 1),
+            )
+
+        def hidden(e, words, scales, c0, h_bf, bank):
             cols = slice(c0, c0 + BLOCK)
-            acc = hid_psum.tile([P, PACK, BLOCK], F32, name="acc")
+            acc = hid_psum.tile([P, PACK, BLOCK], F32, name="acc", tag="bank%d" % (bank % 4))
             for t in range(PACK):
-                w_cols = slice((t % 2) * P, (t % 2 + 1) * P)
                 for o in range(PASSES):
-                    nc.tensor.matmul_mx(
-                        out=acc[:, t, :],
-                        lhsT=w1_code[e, o, t // 2][:, w_cols].bitcast(FP8X4),
-                        lhsT_scale=w1_scale[e, o, t // 2][:, w_cols],
-                        rhs=words[o][:, cols].bitcast(FP8X4),
-                        rhs_scale=scales[4 * o : P, cols],
-                        start=(o == 0),
-                        stop=(o == PASSES - 1),
-                    )
+                    first_matmul(e, t, o, acc[:, t, :], words, scales, cols)
             nc.scalar.activation(h_bf, acc[:].rearrange("p t s -> p s t"), SILU)
 
         def shared_hidden(block, h_bf):
-            hidden(SHARED, x_word, x_scale, block * BLOCK, h_bf)
+            hidden(SHARED, x_word, x_scale, block * BLOCK, h_bf, block)
 
         def routed_hidden(e, h_bf):
-            hidden(e, slot_word, slot_scale, e * C, h_bf)
+            hidden(e, slot_word, slot_scale, e * C, h_bf, T // BLOCK + e)
 
         def h_tile(name, blocks, reuse):
             return sb(name, [P, blocks, BLOCK, PACK], BF16, reuse)
@@ -201,6 +194,18 @@ def tile_moe_shr_mlp_silu_kernel(tc, x_words, x_scales, w1, w2, gate, offs, out)
             picked = offsets[:, e * C // 16 : (e + 1) * C // 16]
             nc.vector.tensor_tensor(routed[:].indirect(picked), y_sb[:], gate_sb[:, e, :], MULT)
 
+        gate_sb = sb("gate_sb", [P, E, C], F32)
+
+        def spread_gate():
+            gate_cols_psum = hid_psum.tile([P, P], F32, name="gate_cols_psum", tag="bank0")
+            nc.tensor.transpose(gate_cols_psum[:], gate_rows[:], identity[:])
+            gate_cols = sb("gate_cols", [P, E], F32)
+            nc.scalar.copy(gate_cols[:], gate_cols_psum[:, 0:E])
+            gate_psum = hid_psum.tile([P, E, C], F32, name="gate_psum", tag="bank1")
+            for e in range(E):
+                nc.tensor.transpose(gate_psum[:, e, :], gate_cols[:, e : e + 1].to_broadcast([P, P]), identity[:])
+            nc.scalar.copy(gate_sb[:], gate_psum[:])
+
         prepare_w1(SHARED, 0)
         prepare_w1(SHARED, 1)
         hs = []
@@ -212,6 +217,8 @@ def tile_moe_shr_mlp_silu_kernel(tc, x_words, x_scales, w1, w2, gate, offs, out)
             waiting = h_tile("hs_bf%d" % o, 2, raw_name(0, o))
             shared_hidden(2 * o, waiting[:, 0, :, :])
             shared_hidden(2 * o + 1, waiting[:, 1, :, :])
+            if o == 0:
+                spread_gate()
         for e in range(LAST - 1):
             prepare_w1(e + 1, 0, vector_alone=(e == 0))
             blocks = 2 if e == 0 else 1
@@ -223,7 +230,7 @@ def tile_moe_shr_mlp_silu_kernel(tc, x_words, x_scales, w1, w2, gate, offs, out)
             code, scale = quantize_h("h%d" % e, h_bf, blocks)
             if e == 0:
                 hs.append((code[:, BLOCK:], scale[:, BLOCK:]))
-            prepare_w2(e)
+            prepare_w2(e, nc.scalar.copy)
             prepare_w1(e + 1, 1)
             routed_output(e, code[:, :C], scale[:, :C], raw_name(e + 1, 1))
 
@@ -231,15 +238,23 @@ def tile_moe_shr_mlp_silu_kernel(tc, x_words, x_scales, w1, w2, gate, offs, out)
         prepare_w1(LAST, 0)
         h_bf = h_tile("h_bf%d" % e, 1, raw_name(LAST, 0))
         routed_hidden(e, h_bf[:, 0, :, :])
+        last_cols = slice(LAST * C, E * C)
+        halves = [hid_psum.tile([P, 2, BLOCK], F32, name="half%d" % pair, tag="bank%d" % pair) for pair in range(2)]
+        for pair in range(2):
+            first_matmul(LAST, 2 * pair, 0, halves[pair][:, 0, :], slot_word, slot_scale, last_cols)
         prepare_w1(LAST, 1)
         code, scale = quantize_h("h%d" % e, h_bf, 1, bf_name(LAST, 1, 1))
-        prepare_w2(e)
+        prepare_w2(e, nc.scalar.copy)
         routed_output(e, code[:], scale[:], None)
-        prepare_w2(LAST)
+        prepare_w2(LAST, nc.scalar.copy)
+        prepare_w2(SHARED, nc.vector.tensor_copy)
         h_bf = h_tile("h_bf%d" % LAST, 1, None)
-        routed_hidden(LAST, h_bf[:, 0, :, :])
+        for pair in range(2):
+            first_matmul(LAST, 2 * pair, 1, halves[pair][:, 0, :], slot_word, slot_scale, last_cols)
+            for o in range(PASSES):
+                first_matmul(LAST, 2 * pair + 1, o, halves[pair][:, 1, :], slot_word, slot_scale, last_cols)
+            nc.scalar.activation(h_bf[:, 0, :, 2 * pair : 2 * pair + 2], halves[pair][:].rearrange("p t s -> p s t"), SILU)
         code, scale = quantize_h("h%d" % LAST, h_bf, 1)
-        prepare_w2(SHARED)
         routed_output(LAST, code[:], scale[:], None)
 
         ys = [ys_psum.tile([P, 4 * BLOCK], F32, name="ys_a"), ys_psum.tile([P, BLOCK], F32, name="ys_b")]

from contextlib import ExitStack

import concourse.mybir as mybir
from concourse.masks import make_identity

K, T, E, C, H, N = 1024, 640, 4, 128, 512, 128
FLOPS = 2 * (E * C + T) * (K * H + H * N)

F32 = mybir.dt.float32
BF16 = mybir.dt.bfloat16
I32 = mybir.dt.int32
U32 = mybir.dt.uint32
U16 = mybir.dt.uint16
U8 = mybir.dt.uint8
FP8X4 = mybir.dt.float8_e4m3fn_x4
SILU = mybir.ActivationFunctionType.Silu
MULT = mybir.AluOpType.mult
ADD = mybir.AluOpType.add

P = 128
PACK = 4
K_PASS = P * PACK
PASSES = K // K_PASS
SHARED = E
LAST = E - 1
BLOCK = 128
GATHER = 256


def tile_moe_shr_mlp_silu_kernel(tc, x_words, x_scales, w1, w2, gate, offs, out):
    nc = tc.nc
    with ExitStack() as ctx:
        keep = ctx.enter_context(tc.tile_pool(name="keep", bufs=1))
        hid_psum = ctx.enter_context(tc.psum_pool(name="hid_psum", bufs=1))
        y_psum = ctx.enter_context(tc.psum_pool(name="y_psum", bufs=2))
        ys_psum = ctx.enter_context(tc.psum_pool(name="ys_psum", bufs=1))

        def sb(name, shape, dtype, reuse=None):
            return keep.tile(shape, dtype, name=name, tag=reuse or name, align_bytes=64)

        offsets = keep.tile([P, E * C // 16], U16, name="offsets")
        x_scale = sb("x_scale", [P, T], U8)
        nc.vector.memset(x_scale[:].bitcast(I32), 0)
        gate_rows = sb("gate_rows", [P, C], F32)
        nc.vector.memset(gate_rows[:], 0.0)
        warm_out = sb("warm_out", [P, 1], F32)
        warm = sb("warm", [P, 1], F32)
        nc.vector.memset(warm[:], 0.0)
        routed = sb("routed", [P, T], F32)
        nc.vector.memset(routed[:], 0.0)
        identity = sb("identity", [P, P], F32)
        make_identity(nc, identity[:])

        x_word = [sb("x_word%d" % o, [P, T], I32) for o in range(PASSES)]

        def load_words(o):
            nc.sync.dma_start(out=x_word[o][:], in_=x_words[o].rearrange("p t r -> p (t r)").bitcast(I32))

        load_words(0)
        nc.sync.dma_start(offsets[:], offs)
        load_words(1)
        for q in range(4):
            nc.scalar.dma_start(
                out=x_scale[32 * q : 32 * q + 4 * PASSES, :].bitcast(I32),
                in_=x_scales[:, 4 * q : 4 * q + 4, :].bitcast(I32),
            )
        nc.scalar.activation(warm_out[:], warm[:], SILU)

        w1_raw = {}
        w2_raw = {}

        def raw_name(e, o):
            return "w1_raw%d_%d" % (e, o)

        def bf_name(e, o, pair):
            return "w1_bf%d_%d_%d" % (e, o, pair)

        def load_w1(e, o):
            w1_raw[e, o] = sb(raw_name(e, o), [P, PACK, H], F32)
            rows = w1[e, o * K_PASS : (o + 1) * K_PASS, :]
            nc.sync.dma_start(out=w1_raw[e, o][:], in_=rows.rearrange("(p j) c -> p j c", j=PACK))

        def load_w2(e):
            w2_raw[e] = sb("w2_raw%d" % e, [P, PACK, N], F32)
            nc.sync.dma_start(out=w2_raw[e][:], in_=w2[e].rearrange("(p j) n -> p j n", j=PACK))

        load_w1(SHARED, 0)
        load_w1(SHARED, 1)
        load_w1(0, 0)
        nc.sync.dma_start(out=gate_rows[0:E, :], in_=gate[0].rearrange("(e c) -> e c", c=C))
        load_w1(0, 1)
        for e in range(1, LAST):
            load_w1(e, 0)
            load_w2(e - 1)
            load_w1(e, 1)
        load_w1(LAST, 0)
        load_w1(LAST, 1)
        for e in (LAST - 1, LAST, SHARED):
            load_w2(e)

        slot_word = [sb("slot_word%d" % o, [P, E * C], U32) for o in range(PASSES)]
        slot_scale = sb("slot_scale", [P, E * C], U8)
        for window, gathered in ((x_word[0][:].bitcast(U32), slot_word[0]), (x_word[1][:].bitcast(U32), slot_word[1]), (x_scale[:], slot_scale)):
            for s0 in range(0, E * C, GATHER):
                picked = offsets[:, s0 // 16 : (s0 + GATHER) // 16]
                nc.vector.tensor_copy(gathered[:, s0 : s0 + GATHER], window.indirect(picked))

        def quantize(code, scale, values):
            nc.vector.quantize_mx(out=code.bitcast(FP8X4), scales=scale, in_=values)

        w1_code = {}
        w1_scale = {}

        def prepare_w1(e, o, vector_alone=False):
            grouped = []
            for pair in range(2):
                g = sb(bf_name(e, o, pair), [P, 2, P, PACK], BF16)
                src = w1_raw[e, o][:].rearrange("p j (m t) -> p m j t", t=PACK)[:, :, :, 2 * pair : 2 * pair + 2]
                dst = g[:].rearrange("p t m j -> p m j t")
                if pair == 0 or vector_alone:
                    nc.vector.tensor_copy(dst, src)
                else:
                    nc.scalar.copy(dst, src)
                grouped.append(g)
            for pair in range(2):
                w1_code[e, o, pair] = sb("w1_code%d_%d_%d" % (e, o, pair), [P, 2 * P], U32)
                w1_scale[e, o, pair] = sb("w1_scale%d_%d_%d" % (e, o, pair), [P, 2 * P], U8)
                values = grouped[pair][:].rearrange("p t m j -> p (t m j)")
                quantize(w1_code[e, o, pair][:], w1_scale[e, o, pair][:], values)

        w2_code = {}
        w2_scale = {}

        def prepare_w2(e, copy):
            g = sb("w2_bf%d" % e, [P, N, PACK], BF16)
            dst = g[:].rearrange("p (c i) j -> p c j i", i=4)
            src = w2_raw[e][:].rearrange("p j (c i) -> p c j i", i=4)
            copy(dst, src)
            w2_code[e] = sb("w2_code%d" % e, [P, N], U32)
            w2_scale[e] = sb("w2_scale%d" % e, [P, N], U8)
            quantize(w2_code[e][:], w2_scale[e][:], g[:].rearrange("p n j -> p (n j)"))

        def first_matmul(e, t, o, acc, words, scales, cols):
            w_cols = slice((t % 2) * P, (t % 2 + 1) * P)
            nc.tensor.matmul_mx(
                out=acc,
                lhsT=w1_code[e, o, t // 2][:, w_cols].bitcast(FP8X4),
                lhsT_scale=w1_scale[e, o, t // 2][:, w_cols],
                rhs=words[o][:, cols].bitcast(FP8X4),
                rhs_scale=scales[4 * o : P, cols],
                start=(o == 0),
                stop=(o == PASSES - 1),
            )

        def hidden(e, words, scales, c0, h_bf, bank):
            cols = slice(c0, c0 + BLOCK)
            acc = hid_psum.tile([P, PACK, BLOCK], F32, name="acc", tag="bank%d" % (bank % 4))
            for t in range(PACK):
                for o in range(PASSES):
                    first_matmul(e, t, o, acc[:, t, :], words, scales, cols)
            nc.scalar.activation(h_bf, acc[:].rearrange("p t s -> p s t"), SILU)

        def shared_hidden(block, h_bf):
            hidden(SHARED, x_word, x_scale, block * BLOCK, h_bf, block)

        def routed_hidden(e, h_bf):
            hidden(e, slot_word, slot_scale, e * C, h_bf, T // BLOCK + e)

        def h_tile(name, blocks, reuse):
            return sb(name, [P, blocks, BLOCK, PACK], BF16, reuse)

        def quantize_h(name, h_bf, blocks, reuse=None):
            code = sb(name + "_code", [P, blocks * BLOCK], U32, reuse)
            scale = sb(name + "_scale", [P, blocks * BLOCK], U8)
            quantize(code[:], scale[:], h_bf[:].rearrange("p b s t -> p (b s t)"))
            return code, scale

        def second_matmul(e, y, h_code, h_scale):
            nc.tensor.matmul_mx(
                out=y,
                lhsT=w2_code[e][:].bitcast(FP8X4),
                lhsT_scale=w2_scale[e][:],
                rhs=h_code.bitcast(FP8X4),
                rhs_scale=h_scale,
                start=True,
                stop=True,
            )

        def routed_output(e, h_code, h_scale, reuse):
            y = y_psum.tile([P, C], F32, name="y")
            second_matmul(e, y[:], h_code, h_scale)
            y_sb = sb("y_sb%d" % e, [P, C], F32, reuse)
            nc.scalar.copy(y_sb[:], y[:])
            picked = offsets[:, e * C // 16 : (e + 1) * C // 16]
            nc.vector.tensor_tensor(routed[:].indirect(picked), y_sb[:], gate_sb[:, e, :], MULT)

        gate_sb = sb("gate_sb", [P, E, C], F32)

        def spread_gate():
            gate_cols_psum = hid_psum.tile([P, P], F32, name="gate_cols_psum", tag="bank0")
            nc.tensor.transpose(gate_cols_psum[:], gate_rows[:], identity[:])
            gate_cols = sb("gate_cols", [P, E], F32)
            nc.scalar.copy(gate_cols[:], gate_cols_psum[:, 0:E])
            gate_psum = hid_psum.tile([P, E, C], F32, name="gate_psum", tag="bank1")
            for e in range(E):
                nc.tensor.transpose(gate_psum[:, e, :], gate_cols[:, e : e + 1].to_broadcast([P, P]), identity[:])
            nc.scalar.copy(gate_sb[:], gate_psum[:])

        prepare_w1(SHARED, 0)
        prepare_w1(SHARED, 1)
        hs = []
        waiting = None
        for o in range(PASSES):
            prepare_w1(0, o, vector_alone=(o == 1))
            if waiting is not None:
                hs.append(quantize_h("hs%d" % (o - 1), waiting, 2, bf_name(0, o, 1)))
            waiting = h_tile("hs_bf%d" % o, 2, raw_name(0, o))
            shared_hidden(2 * o, waiting[:, 0, :, :])
            shared_hidden(2 * o + 1, waiting[:, 1, :, :])
            if o == 0:
                spread_gate()
        for e in range(LAST - 1):
            prepare_w1(e + 1, 0, vector_alone=(e == 0))
            blocks = 2 if e == 0 else 1
            h_bf = h_tile("h_bf%d" % e, blocks, raw_name(e + 1, 0))
            if e == 0:
                hs.append(quantize_h("hs1", waiting, 2, bf_name(1, 0, 1)))
                shared_hidden(4, h_bf[:, 1, :, :])
            routed_hidden(e, h_bf[:, 0, :, :])
            code, scale = quantize_h("h%d" % e, h_bf, blocks)
            if e == 0:
                hs.append((code[:, BLOCK:], scale[:, BLOCK:]))
            prepare_w2(e, nc.scalar.copy)
            prepare_w1(e + 1, 1)
            routed_output(e, code[:, :C], scale[:, :C], raw_name(e + 1, 1))

        e = LAST - 1
        prepare_w1(LAST, 0)
        h_bf = h_tile("h_bf%d" % e, 1, raw_name(LAST, 0))
        routed_hidden(e, h_bf[:, 0, :, :])
        last_cols = slice(LAST * C, E * C)
        halves = [hid_psum.tile([P, 2, BLOCK], F32, name="half%d" % pair, tag="bank%d" % pair) for pair in range(2)]
        for pair in range(2):
            first_matmul(LAST, 2 * pair, 0, halves[pair][:, 0, :], slot_word, slot_scale, last_cols)
        prepare_w1(LAST, 1)
        code, scale = quantize_h("h%d" % e, h_bf, 1, bf_name(LAST, 1, 1))
        prepare_w2(e, nc.scalar.copy)
        routed_output(e, code[:], scale[:], None)
        prepare_w2(LAST, nc.scalar.copy)
        prepare_w2(SHARED, nc.vector.tensor_copy)
        h_bf = h_tile("h_bf%d" % LAST, 1, None)
        for pair in range(2):
            first_matmul(LAST, 2 * pair, 1, halves[pair][:, 0, :], slot_word, slot_scale, last_cols)
            for o in range(PASSES):
                first_matmul(LAST, 2 * pair + 1, o, halves[pair][:, 1, :], slot_word, slot_scale, last_cols)
            nc.scalar.activation(h_bf[:, 0, :, 2 * pair : 2 * pair + 2], halves[pair][:].rearrange("p t s -> p s t"), SILU)
        code, scale = quantize_h("h%d" % LAST, h_bf, 1)
        routed_output(LAST, code[:], scale[:], None)

        ys = [ys_psum.tile([P, 4 * BLOCK], F32, name="ys_a"), ys_psum.tile([P, BLOCK], F32, name="ys_b")]
        pieces = [(0, ys[0][:, : 2 * BLOCK]), (2 * BLOCK, ys[0][:, 2 * BLOCK :]), (4 * BLOCK, ys[1][:])]
        for (c0, y), (code, scale) in zip(pieces, hs):
            second_matmul(SHARED, y, code[:], scale[:])
        for piece, (c0, y) in enumerate(pieces):
            width = y.shape[1]
            result = sb("result%d" % piece, [P, width], F32)
            nc.vector.tensor_tensor(result[:], y, routed[:, c0 : c0 + width], ADD)
            queue = nc.scalar if piece == 1 else nc.sync
            queue.dma_start(out=out[:, c0 : c0 + width], in_=result[:])
